import numpy as np
import ml_dtypes


def mxq(x, axis, fmt="e4m3"):
    dtype, down = {"e4m3": (ml_dtypes.float8_e4m3fn, 7), "e5m2": (ml_dtypes.float8_e5m2, 14)}[fmt]
    v = np.moveaxis(np.asarray(x, np.float32).astype(ml_dtypes.bfloat16).astype(np.float64), axis, -1)
    blocks = v.reshape(v.shape[:-1] + (-1, 32))
    amax = np.abs(blocks).max(-1, keepdims=True)
    byte = np.maximum(np.where(amax > 0, np.frexp(amax)[1] - 1 + 127, 0) - down, 1)
    scale = np.exp2(byte - 127.0)
    codes = (blocks / scale).astype(np.float32).astype(dtype).astype(np.float64)
    return np.moveaxis((codes * scale).reshape(v.shape), -1, axis)


WIDE = False


def mx_kscale(k):
    if not WIDE:
        return np.ones(k)
    levels = np.array([10, -10, 5, -5, 0])
    if k % 512:
        return np.exp2(np.random.permutation(np.resize(levels, k // 32))).repeat(32)
    a = np.empty((k // 512, 16))
    for p in range(k // 512):
        a[p, :8] = np.random.permutation(np.resize(levels, 8))
        for g in range(8):
            far = levels[np.abs(levels - a[p, g]) >= 10]
            a[p, g + 8] = far[np.random.randint(len(far))]
    return np.exp2(a.ravel()).repeat(32)


def f64(x):
    return np.asarray(x).astype(np.float64)


def striped(idx):
    return np.tile(idx.reshape(-1, 16).T, (8, 1)).astype(np.uint16)


def unstriped(offs):
    return offs[:16].T.reshape(-1).astype(np.int64)


def striped8(idx):
    return np.concatenate([x.reshape(-1, 16).T for x in idx]).astype(np.uint16)


def runs(offs, k):
    lists = np.stack([offs[16 * r : 16 * r + 16].T.reshape(-1) for r in range(8)]).astype(np.int64)
    return lists[np.arange(k) % 512 // 64]


def pack_weight(w):
    k, n = w.shape
    w = f64(np.asarray(w, np.float32).astype(ml_dtypes.bfloat16)).reshape(k // 32, 32, n)
    amax = np.abs(w).max(1)
    byte = np.clip(np.where(amax > 0, np.frexp(amax)[1] - 1 + 127 - 7, 1), 1, 254)
    scaled = (w * np.exp2(127.0 - byte)[:, None, :]).reshape(k, n).astype(np.float32)
    words = np.ascontiguousarray(scaled.reshape(k // 512, 128, 4, n).transpose(0, 1, 3, 2)).astype(ml_dtypes.float8_e4m3fn).view(np.uint8)
    return words, np.ascontiguousarray(byte.astype(np.uint8).reshape(k // 512, 16, n))


def unpack_weight(words, scales):
    g, p, n, _ = words.shape
    vals = np.ascontiguousarray(words).view(ml_dtypes.float8_e4m3fn).astype(np.float64) * np.repeat(np.exp2(scales.astype(np.float64) - 127.0), 8, axis=1)[..., None]
    return vals.transpose(0, 1, 3, 2).reshape(g * 512, n)


K, T, S, H, W, G = 512, 1024, 256, 512, 128, 2048


def setup_inputs():
    n = np.random.standard_normal
    s = mx_kscale(K)[:, None]
    packed_xT = pack_weight(n((K, T)) * s)
    packed_w1 = pack_weight(n((K, H)) / np.sqrt(2 * K) / s)
    packed_w2 = pack_weight(n((K, H)) / np.sqrt(2 * K) / s)
    packed_dT = pack_weight(n((K, G)) / s)
    perm = np.random.permutation(S)
    return {
        "x_words": packed_xT[0],
        "x_scales": packed_xT[1],
        "w1_words": packed_w1[0],
        "w1_scales": packed_w1[1],
        "w2_words": packed_w2[0],
        "w2_scales": packed_w2[1],
        "gs": (np.random.uniform(0.5, 1.5, (K, 1)) * s).astype(np.float32),
        "d_words": packed_dT[0],
        "d_scales": packed_dT[1],
        "offs": striped8(np.random.randint(0, T, (8, S))),
        "hz": striped8(np.random.randint(0, T, (8, S))),
        "n1": striped(perm[:W]),
        "n2": striped(perm[W:]),
        "k1": striped8(np.random.randint(0, G, (8, H))),
        "n3": striped(np.random.permutation(S)),
        "n4": striped(np.random.permutation(S)),
    }


def reference(x_words, x_scales, w1_words, w1_scales, w2_words, w2_scales, gs, d_words, d_scales, offs, hz, n1, n2, k1, n3, n4):
    d_k1 = unpack_weight(d_words, d_scales)[np.arange(K)[:, None], runs(k1, K)]
    xq = unpack_weight(x_words, x_scales)[np.arange(K)[:, None], runs(offs, K)]
    x_hz = unpack_weight(x_words, x_scales)[np.arange(K)[:, None], runs(hz, K)]
    y = unpack_weight(w1_words, w1_scales).T @ xq + unpack_weight(w2_words, w2_scales).T @ x_hz
    pa = y[:, unstriped(n1)]
    pb = y[:, unstriped(n2)]
    ra = np.maximum(pa, pb)
    ds = y.copy()
    ds[:, unstriped(n1)] = ra
    z = f64(gs) * ds
    h = 0.0625 * ((d_k1.T @ mxq(z, 0, "e4m3")))
    ds2 = np.zeros((H, S))
    ds2[:, unstriped(n3)] = h
    ds3 = np.zeros((H, S))
    ds3[:, unstriped(n4)] = h
    return np.maximum(ds2, ds3)

@@ -1,0 +1,219 @@
+from contextlib import ExitStack
+
+import concourse.mybir as mybir
+
+FLOPS = 402653184
+
+F32 = mybir.dt.float32
+BF16 = mybir.dt.bfloat16
+I32 = mybir.dt.int32
+U32 = mybir.dt.uint32
+U16 = mybir.dt.uint16
+U8 = mybir.dt.uint8
+FP8X4 = mybir.dt.float8_e4m3fn_x4
+COPY = mybir.ActivationFunctionType.Copy
+MULT = mybir.AluOpType.mult
+MAX = mybir.AluOpType.max
+
+P = 128
+PACK = 4
+T, S, H, W, G = 1024, 256, 512, 128, 2048
+TILES = H // P
+
+
+def words_of(dram_words):
+    return dram_words[0].rearrange("p n t -> p (n t)").bitcast(I32)
+
+
+def tile_picked_dhqfillsendtwo_none_p_kernel(
+    tc, x_words, x_scales, w1_words, w1_scales, w2_words, w2_scales, gs, d_words, d_scales,
+    offs, hz, n1, n2, k1, n3, n4, out,
+):
+    nc = tc.nc
+    with ExitStack() as ctx:
+        lists = ctx.enter_context(tc.tile_pool(name="lists", bufs=1))
+        keep = ctx.enter_context(tc.tile_pool(name="keep", bufs=1))
+        shared = ctx.enter_context(tc.tile_pool(name="shared", bufs=1))
+        psum = ctx.enter_context(tc.psum_pool(name="psum", bufs=1))
+
+        def load_list(dram, name):
+            tile = lists.tile(list(dram.shape), U16, name=name)
+            nc.sync.dma_start(tile[:], dram)
+            return tile
+
+        def sbuf(shape, dtype, name, tag=None):
+            return keep.tile(shape, dtype, name=name, tag=tag or name, align_bytes=64)
+
+        x_word_table = shared.tile([P, T], U32, name="x_word_table", offset=0, align_bytes=64)
+        x_byte_table = sbuf([P, T], U8, "x_byte_table")
+        w_bytes = sbuf([P, H], U8, "w_bytes")
+        w_words = [sbuf([P, H], U32, "w_words%d" % a) for a in range(2)]
+        gain = sbuf([P, PACK], F32, "gain")
+
+        def load_w_scale_row(queue, a, j):
+            rows = (w1_scales, w2_scales)[a][0].bitcast(I32).rearrange("(q j) n -> j q n", j=4)[j]
+            queue.dma_start(
+                w_bytes[:].bitcast(I32)[4 * a + j : P : 8, :],
+                rows.unsqueeze(1).to_broadcast([4, 4, H // 4]),
+            )
+
+        def load_byte_table(queue, table, scales):
+            for e in range(2):
+                rows = scales[0].bitcast(I32).rearrange("(g e) n -> e g n", e=2)[e]
+                queue.dma_start(
+                    table[:].bitcast(I32)[e:P:2, :],
+                    rows.unsqueeze(1).to_broadcast([8, 8, rows.shape[1]]),
+                )
+
+        w_rows = [(a, j) for a in range(2) for j in range(4)]
+
+        offs_t = load_list(offs, "offs")
+        hz_t = load_list(hz, "hz")
+        load_byte_table(nc.sync, x_byte_table, x_scales)
+        for a, j in w_rows[:3]:
+            load_w_scale_row(nc.sync, a, j)
+        nc.sync.dma_start(x_word_table[:].bitcast(I32), words_of(x_words))
+        for a, j in w_rows[3:]:
+            load_w_scale_row(nc.sync, a, j)
+        k1_t = load_list(k1, "k1")
+        n1_t = load_list(n1, "n1")
+        nc.gpsimd.dma_start(w_words[0][:].bitcast(I32), words_of(w1_words))
+        nc.gpsimd.dma_start(w_words[1][:].bitcast(I32), words_of(w2_words))
+        n2_t = load_list(n2, "n2")
+        n3_t = load_list(n3, "n3")
+        n4_t = load_list(n4, "n4")
+        d_byte_table = shared.tile([P, G], U8, name="d_byte_table", offset=4 * G, align_bytes=64)
+        load_byte_table(nc.gpsimd, d_byte_table, d_scales)
+        nc.gpsimd.dma_start(gain[:], gs.rearrange("(p t) o -> p (t o)", t=PACK))
+
+        def place_scale_rows(queue, picked, name, width):
+            plane = sbuf([P, width], U8, name)
+            nc.vector.tensor_copy(plane[:].bitcast(I32), picked[:].bitcast(I32))
+            for e in range(2):
+                queue.dma_start(plane[:].bitcast(I32)[2 + e : P : 32, :], picked[:].bitcast(I32)[16 + e : P : 32, :])
+            return plane
+
+        x_bytes_picked = sbuf([P, 2 * S], U8, "x_bytes_picked")
+        x_codes = sbuf([P, 2 * S], U32, "x_codes")
+        for a, lst in enumerate((offs_t, hz_t)):
+            nc.vector.tensor_copy(x_bytes_picked[:, a * S : (a + 1) * S], x_byte_table[:].indirect(lst[:]))
+        x_plane = place_scale_rows(nc.scalar, x_bytes_picked, "x_plane", 2 * S)
+        for a, lst in enumerate((offs_t, hz_t)):
+            nc.vector.tensor_copy(x_codes[:, a * S : (a + 1) * S], x_word_table[:].indirect(lst[:]))
+
+        w_plane = sbuf([P, H], U8, "w_plane")
+        nc.vector.tensor_copy(
+            w_plane[:].rearrange("p (t m) -> p t m", t=PACK), w_bytes[:].rearrange("p (m t) -> p t m", t=PACK)
+        )
+        d_word_table = shared.tile([P, G], U32, name="d_word_table", offset=0, align_bytes=64)
+        nc.sync.dma_start(d_word_table[:].bitcast(I32), words_of(d_words))
+
+        w_codes = [[sbuf([P, P], U32, "w_codes%d_%d" % (a, t)) for t in range(PACK)] for a in range(2)]
+        y_bank = [psum.tile([P, S], F32, name="y_bank%d" % t, tag="y_bank%d" % t) for t in range(PACK)]
+        y = [sbuf([P, S], F32, "y%d" % t) for t in range(PACK)]
+        for t in range(PACK):
+            for a in range(2):
+                nc.scalar.copy(w_codes[a][t][:], w_words[a][:, t:H:PACK])
+        for t in range(PACK):
+            for a in range(2):
+                nc.tensor.matmul_mx(
+                    out=y_bank[t][:],
+                    lhsT=w_codes[a][t][:].bitcast(FP8X4),
+                    lhsT_scale=w_plane[4 * a :, t * P : (t + 1) * P],
+                    rhs=x_codes[:, a * S : (a + 1) * S].bitcast(FP8X4),
+                    rhs_scale=x_plane[:, a * S : (a + 1) * S],
+                    start=(a == 0),
+                    stop=(a == 1),
+                )
+        nc.scalar.copy(y[0][:], y_bank[0][:])
+        for t in range(1, PACK):
+            nc.vector.tensor_copy(y[t][:], y_bank[t][:])
+
+        d_bytes_picked = sbuf([P, H], U8, "d_bytes_picked")
+        d_codes = sbuf([P, H], U32, "d_codes")
+        half = H // 2
+
+        def pick_dictionary():
+            for b in range(2):
+                nc.vector.tensor_copy(
+                    d_bytes_picked[:, b * half : (b + 1) * half],
+                    d_byte_table[:].indirect(k1_t[:, b * half // 16 : (b + 1) * half // 16]),
+                )
+            plane = place_scale_rows(nc.sync, d_bytes_picked, "d_plane", H)
+            for b in range(2):
+                nc.vector.tensor_copy(
+                    d_codes[:, b * half : (b + 1) * half],
+                    d_word_table[:].indirect(k1_t[:, b * half // 16 : (b + 1) * half // 16]),
+                )
+            return plane
+
+        ra = []
+        for t in range(PACK):
+            pa = sbuf([P, W], F32, "pa%d" % t)
+            pb = sbuf([P, W], F32, "pb%d" % t)
+            nc.scalar.activation(pa[:], y[t][:].indirect(n1_t[:]), COPY)
+            nc.scalar.activation(pb[:], y[t][:].indirect(n2_t[:]), COPY)
+            if t == 1:
+                d_plane = pick_dictionary()
+                ra.append(shared.tile([P, W], F32, name="ra1", offset=4 * G - 2 * W, align_bytes=64))
+            else:
+                ra.append(sbuf([P, W], F32, "ra%d" % t))
+            nc.vector.tensor_tensor(ra[t][:], pa[:], pb[:], MAX)
+
+        halves = [slice(0, S // 2), slice(S // 2, S)]
+        z = [
+            shared.tile([P, S // 2, PACK], BF16, name="z%d" % b, offset=b * S * PACK, align_bytes=64) for b in range(2)
+        ]
+        for t in range(PACK):
+            nc.scalar.activation(y[t][:].indirect(n1_t[:]), ra[t][:], COPY)
+            for b in range(2):
+                nc.vector.tensor_scalar(z[b][:, :, t], y[t][:, halves[b]], gain[:, t : t + 1], None, MULT)
+        z_codes = sbuf([P, S], U32, "z_codes")
+        z_plane = sbuf([P, S], U8, "z_plane")
+        for b in range(2):
+            nc.vector.quantize_mx(
+                out=z_codes[:, halves[b]].bitcast(FP8X4),
+                scales=z_plane[:, halves[b]],
+                in_=z[b][:].rearrange("p s t -> p (s t)"),
+            )
+
+        def coded_product(u, bank, places):
+            cols = slice(u * P, (u + 1) * P)
+            nc.tensor.matmul_mx(
+                out=bank,
+                lhsT=d_codes[:, cols].bitcast(FP8X4),
+                lhsT_scale=d_plane[:, cols],
+                rhs=z_codes[:, places].bitcast(FP8X4),
+                rhs_scale=z_plane[:, places],
+                start=True,
+                stop=True,
+            )
+
+        for u in range(TILES):
+            h = sbuf([P, S], F32, "h%d" % u)
+            sent3 = sbuf([P, 2 * S], F32, "sent3_%d" % u)
+            sent4 = sbuf([P, 2 * S], F32, "sent4_%d" % u)
+            if u == 0:
+                for b in range(2):
+                    bank = psum.tile([P, S], F32, name="h_first%d" % b, tag="y_bank%d" % b)
+                    coded_product(u, bank[:, : S // 2], halves[b])
+                    if b == 0:
+                        nc.scalar.activation(h[:, halves[b]], bank[:, : S // 2], COPY, scale=0.0625)
+                    else:
+                        nc.vector.tensor_scalar(h[:, halves[b]], bank[:, : S // 2], 0.0625, None, MULT)
+                    nc.scalar.activation(sent3[:].indirect(n3_t[:, b * 8 : (b + 1) * 8]), h[:, halves[b]], COPY)
+            else:
+                bank = psum.tile([P, S], F32, name="h_bank%d" % u)
+                coded_product(u, bank[:], slice(0, S))
+                nc.vector.tensor_scalar(h[:], bank[:], 0.0625, None, MULT)
+                nc.scalar.activation(sent3[:].indirect(n3_t[:]), h[:], COPY)
+            nc.scalar.activation(sent4[:].indirect(n4_t[:]), h[:], COPY)
+            larger = sbuf([P, S], F32, "larger%d" % u)
+            rows = out[u * P : (u + 1) * P, :]
+            if u < TILES - 1:
+                nc.vector.tensor_tensor(larger[:], sent3[:, :S], sent4[:, :S], MAX)
+                nc.sync.dma_start(rows, larger[:])
+            else:
+                for b, queue in enumerate((nc.sync, nc.scalar)):
+                    nc.vector.tensor_tensor(larger[:, halves[b]], sent3[:, halves[b]], sent4[:, halves[b]], MAX)
+                    queue.dma_start(rows[:, halves[b]], larger[:, halves[b]])

@@ -44,18 +44,10 @@ def tile_picked_dhqfillsendtwo_none_p_kernel(
         def sbuf(shape, dtype, name, tag=None):
             return keep.tile(shape, dtype, name=name, tag=tag or name, align_bytes=64)
 
-        x_word_table = shared.tile([P, T], U32, name="x_word_table", offset=0, align_bytes=64)
+        x_word_table = shared.tile([P, T], U32, name="x_word_table", offset=4 * G - 2 * T, align_bytes=64)
         x_byte_table = sbuf([P, T], U8, "x_byte_table")
-        w_bytes = sbuf([P, H], U8, "w_bytes")
+        w_bytes = sbuf([P, 2 * H], U8, "w_bytes", tag="w_then_d_bytes")
         w_words = [sbuf([P, H], U32, "w_words%d" % a) for a in range(2)]
-        gain = sbuf([P, PACK], F32, "gain")
-
-        def load_w_scale_row(queue, a, j):
-            rows = (w1_scales, w2_scales)[a][0].bitcast(I32).rearrange("(q j) n -> j q n", j=4)[j]
-            queue.dma_start(
-                w_bytes[:].bitcast(I32)[4 * a + j : P : 8, :],
-                rows.unsqueeze(1).to_broadcast([4, 4, H // 4]),
-            )
 
         def load_byte_table(queue, table, scales):
             for e in range(2):
@@ -65,48 +57,50 @@ def tile_picked_dhqfillsendtwo_none_p_kernel(
                     rows.unsqueeze(1).to_broadcast([8, 8, rows.shape[1]]),
                 )
 
-        w_rows = [(a, j) for a in range(2) for j in range(4)]
-
+        load_byte_table(nc.sync, x_byte_table, x_scales)
         offs_t = load_list(offs, "offs")
         hz_t = load_list(hz, "hz")
-        load_byte_table(nc.sync, x_byte_table, x_scales)
-        for a, j in w_rows[:3]:
-            load_w_scale_row(nc.sync, a, j)
-        nc.sync.dma_start(x_word_table[:].bitcast(I32), words_of(x_words))
-        for a, j in w_rows[3:]:
-            load_w_scale_row(nc.sync, a, j)
-        k1_t = load_list(k1, "k1")
+        w_rows = w_bytes[:].bitcast(I32)
+        for a, scales in enumerate((w1_scales, w2_scales)):
+            nc.sync.dma_start(
+                w_rows[:, a * H // 4 : (a + 1) * H // 4],
+                scales[0].bitcast(I32).unsqueeze(1).to_broadcast([16, 8, H // 4]),
+            )
         n1_t = load_list(n1, "n1")
-        nc.gpsimd.dma_start(w_words[0][:].bitcast(I32), words_of(w1_words))
-        nc.gpsimd.dma_start(w_words[1][:].bitcast(I32), words_of(w2_words))
         n2_t = load_list(n2, "n2")
+        k1_t = load_list(k1, "k1")
         n3_t = load_list(n3, "n3")
         n4_t = load_list(n4, "n4")
-        d_byte_table = shared.tile([P, G], U8, name="d_byte_table", offset=4 * G, align_bytes=64)
-        load_byte_table(nc.gpsimd, d_byte_table, d_scales)
-        nc.gpsimd.dma_start(gain[:], gs.rearrange("(p t) o -> p (t o)", t=PACK))
+        for j in range(1, 4):
+            nc.sync.dma_start(w_rows[j:P:32, :], w_rows[8 * j : P : 32, :])
+        nc.gpsimd.dma_start(x_word_table[:].bitcast(I32), words_of(x_words))
+        nc.gpsimd.dma_start(w_words[0][:].bitcast(I32), words_of(w1_words))
+        nc.gpsimd.dma_start(w_words[1][:].bitcast(I32), words_of(w2_words))
 
         def place_scale_rows(queue, picked, name, width):
             plane = sbuf([P, width], U8, name)
             nc.vector.tensor_copy(plane[:].bitcast(I32), picked[:].bitcast(I32))
             for e in range(2):
-                queue.dma_start(plane[:].bitcast(I32)[2 + e : P : 32, :], picked[:].bitcast(I32)[16 + e : P : 32, :])
+                queue.dma_start(plane[:].bitcast(I32)[2 + e : P : 32, :], plane[:].bitcast(I32)[16 + e : P : 32, :])
             return plane
 
-        x_bytes_picked = sbuf([P, 2 * S], U8, "x_bytes_picked")
-        x_codes = sbuf([P, 2 * S], U32, "x_codes")
+        x_bytes_picked = sbuf([P, 2 * S], U8, "x_bytes_picked", tag="x_picked")
         for a, lst in enumerate((offs_t, hz_t)):
             nc.vector.tensor_copy(x_bytes_picked[:, a * S : (a + 1) * S], x_byte_table[:].indirect(lst[:]))
-        x_plane = place_scale_rows(nc.scalar, x_bytes_picked, "x_plane", 2 * S)
+        x_plane = place_scale_rows(nc.sync, x_bytes_picked, "x_plane", 2 * S)
+        x_codes = sbuf([P, 2 * S], U32, "x_codes", tag="x_picked")
         for a, lst in enumerate((offs_t, hz_t)):
             nc.vector.tensor_copy(x_codes[:, a * S : (a + 1) * S], x_word_table[:].indirect(lst[:]))
 
-        w_plane = sbuf([P, H], U8, "w_plane")
-        nc.vector.tensor_copy(
-            w_plane[:].rearrange("p (t m) -> p t m", t=PACK), w_bytes[:].rearrange("p (m t) -> p t m", t=PACK)
-        )
+        w_plane = [sbuf([P, 2, P], U8, "w_plane%d" % t) for t in range(PACK)]
+        for t in range(PACK):
+            nc.vector.tensor_copy(w_plane[t][:], w_bytes[:].rearrange("p (a m t) -> p t a m", a=2, t=PACK)[:, t])
+        d_byte_table = shared.tile([P, G], U8, name="d_byte_table", offset=4 * G + 64, align_bytes=64)
+        load_byte_table(nc.sync, d_byte_table, d_scales)
         d_word_table = shared.tile([P, G], U32, name="d_word_table", offset=0, align_bytes=64)
         nc.sync.dma_start(d_word_table[:].bitcast(I32), words_of(d_words))
+        gain = shared.tile([P, PACK], F32, name="gain", offset=4 * G, align_bytes=64)
+        nc.sync.dma_start(gain[:], gs.rearrange("(p t) o -> p (t o)", t=PACK))
 
         w_codes = [[sbuf([P, P], U32, "w_codes%d_%d" % (a, t)) for t in range(PACK)] for a in range(2)]
         y_bank = [psum.tile([P, S], F32, name="y_bank%d" % t, tag="y_bank%d" % t) for t in range(PACK)]
@@ -119,7 +113,7 @@ def tile_picked_dhqfillsendtwo_none_p_kernel(
                 nc.tensor.matmul_mx(
                     out=y_bank[t][:],
                     lhsT=w_codes[a][t][:].bitcast(FP8X4),
-                    lhsT_scale=w_plane[4 * a :, t * P : (t + 1) * P],
+                    lhsT_scale=w_plane[t][:, a, :],
                     rhs=x_codes[:, a * S : (a + 1) * S].bitcast(FP8X4),
                     rhs_scale=x_plane[:, a * S : (a + 1) * S],
                     start=(a == 0),
@@ -129,7 +123,7 @@ def tile_picked_dhqfillsendtwo_none_p_kernel(
         for t in range(1, PACK):
             nc.vector.tensor_copy(y[t][:], y_bank[t][:])
 
-        d_bytes_picked = sbuf([P, H], U8, "d_bytes_picked")
+        d_bytes_picked = sbuf([P, H], U8, "d_bytes_picked", tag="w_then_d_bytes")
         d_codes = sbuf([P, H], U32, "d_codes")
         half = H // 2
 
@@ -153,9 +147,9 @@ def tile_picked_dhqfillsendtwo_none_p_kernel(
             pb = sbuf([P, W], F32, "pb%d" % t)
             nc.scalar.activation(pa[:], y[t][:].indirect(n1_t[:]), COPY)
             nc.scalar.activation(pb[:], y[t][:].indirect(n2_t[:]), COPY)
-            if t == 1:
+            if t == 2:
                 d_plane = pick_dictionary()
-                ra.append(shared.tile([P, W], F32, name="ra1", offset=4 * G - 2 * W, align_bytes=64))
+                ra.append(shared.tile([P, W], F32, name="ra2", offset=4 * G - 4 * W, align_bytes=64))
             else:
                 ra.append(sbuf([P, W], F32, "ra%d" % t))
             nc.vector.tensor_tensor(ra[t][:], pa[:], pb[:], MAX)

@@ -44,51 +44,47 @@ def tile_picked_dhqfillsendtwo_none_p_kernel(
         def sbuf(shape, dtype, name, tag=None):
             return keep.tile(shape, dtype, name=name, tag=tag or name, align_bytes=64)
 
-        x_word_table = shared.tile([P, T], U32, name="x_word_table", offset=4 * G - 2 * T, align_bytes=64)
+        x_word_table = sbuf([P, T], U32, "x_word_table")
         x_byte_table = sbuf([P, T], U8, "x_byte_table")
         w_bytes = sbuf([P, 2 * H], U8, "w_bytes", tag="w_then_d_bytes")
         w_words = [sbuf([P, H], U32, "w_words%d" % a) for a in range(2)]
 
-        def load_byte_table(queue, table, scales):
-            for e in range(2):
-                rows = scales[0].bitcast(I32).rearrange("(g e) n -> e g n", e=2)[e]
-                queue.dma_start(
-                    table[:].bitcast(I32)[e:P:2, :],
-                    rows.unsqueeze(1).to_broadcast([8, 8, rows.shape[1]]),
-                )
+        def load_scale_rows(rows, scales):
+            words = scales[0].bitcast(I32)
+            nc.sync.dma_start(rows.bitcast(I32), words.unsqueeze(1).to_broadcast([16, 8, words.shape[1]]))
 
-        load_byte_table(nc.sync, x_byte_table, x_scales)
+        def place_scale_rows(plane):
+            words = plane[:].bitcast(I32)
+            for j in range(1, 4):
+                nc.sync.dma_start(words[j:P:32, :], words[8 * j : P : 32, :])
+
+        load_scale_rows(x_byte_table[:], x_scales)
         offs_t = load_list(offs, "offs")
         hz_t = load_list(hz, "hz")
-        w_rows = w_bytes[:].bitcast(I32)
-        for a, scales in enumerate((w1_scales, w2_scales)):
-            nc.sync.dma_start(
-                w_rows[:, a * H // 4 : (a + 1) * H // 4],
-                scales[0].bitcast(I32).unsqueeze(1).to_broadcast([16, 8, H // 4]),
-            )
+        load_scale_rows(w_bytes[:, :H], w1_scales)
+        load_scale_rows(w_bytes[:, H:], w2_scales)
         n1_t = load_list(n1, "n1")
         n2_t = load_list(n2, "n2")
+        nc.sync.dma_start(x_word_table[:].bitcast(I32), words_of(x_words))
         k1_t = load_list(k1, "k1")
         n3_t = load_list(n3, "n3")
         n4_t = load_list(n4, "n4")
-        for j in range(1, 4):
-            nc.sync.dma_start(w_rows[j:P:32, :], w_rows[8 * j : P : 32, :])
-        nc.gpsimd.dma_start(x_word_table[:].bitcast(I32), words_of(x_words))
+        place_scale_rows(w_bytes)
         nc.gpsimd.dma_start(w_words[0][:].bitcast(I32), words_of(w1_words))
         nc.gpsimd.dma_start(w_words[1][:].bitcast(I32), words_of(w2_words))
 
-        def place_scale_rows(queue, picked, name, width):
+        def plane_of(picked, name, width):
             plane = sbuf([P, width], U8, name)
-            nc.vector.tensor_copy(plane[:].bitcast(I32), picked[:].bitcast(I32))
-            for e in range(2):
-                queue.dma_start(plane[:].bitcast(I32)[2 + e : P : 32, :], plane[:].bitcast(I32)[16 + e : P : 32, :])
+            nc.vector.tensor_copy(plane[:].bitcast(I32), picked.bitcast(I32))
+            place_scale_rows(plane)
             return plane
 
-        x_bytes_picked = sbuf([P, 2 * S], U8, "x_bytes_picked", tag="x_picked")
+        x_bytes_wide = shared.tile([P, G + 192], U8, name="x_bytes_picked", offset=4 * G - 64, align_bytes=64)
+        x_bytes_picked = x_bytes_wide[:, : 2 * S]
         for a, lst in enumerate((offs_t, hz_t)):
             nc.vector.tensor_copy(x_bytes_picked[:, a * S : (a + 1) * S], x_byte_table[:].indirect(lst[:]))
-        x_plane = place_scale_rows(nc.sync, x_bytes_picked, "x_plane", 2 * S)
-        x_codes = sbuf([P, 2 * S], U32, "x_codes", tag="x_picked")
+        x_plane = plane_of(x_bytes_picked, "x_plane", 2 * S)
+        x_codes = shared.tile([P, 2 * S], U32, name="x_codes", offset=5 * G + 64, align_bytes=64)
         for a, lst in enumerate((offs_t, hz_t)):
             nc.vector.tensor_copy(x_codes[:, a * S : (a + 1) * S], x_word_table[:].indirect(lst[:]))
 
@@ -96,7 +92,7 @@ def tile_picked_dhqfillsendtwo_none_p_kernel(
         for t in range(PACK):
             nc.vector.tensor_copy(w_plane[t][:], w_bytes[:].rearrange("p (a m t) -> p t a m", a=2, t=PACK)[:, t])
         d_byte_table = shared.tile([P, G], U8, name="d_byte_table", offset=4 * G + 64, align_bytes=64)
-        load_byte_table(nc.sync, d_byte_table, d_scales)
+        load_scale_rows(d_byte_table[:], d_scales)
         d_word_table = shared.tile([P, G], U32, name="d_word_table", offset=0, align_bytes=64)
         nc.sync.dma_start(d_word_table[:].bitcast(I32), words_of(d_words))
         gain = shared.tile([P, PACK], F32, name="gain", offset=4 * G, align_bytes=64)
@@ -133,7 +129,7 @@ def tile_picked_dhqfillsendtwo_none_p_kernel(
                     d_bytes_picked[:, b * half : (b + 1) * half],
                     d_byte_table[:].indirect(k1_t[:, b * half // 16 : (b + 1) * half // 16]),
                 )
-            plane = place_scale_rows(nc.sync, d_bytes_picked, "d_plane", H)
+            plane = plane_of(d_bytes_picked[:], "d_plane", H)
             for b in range(2):
                 nc.vector.tensor_copy(
                     d_codes[:, b * half : (b + 1) * half],
@@ -147,12 +143,13 @@ def tile_picked_dhqfillsendtwo_none_p_kernel(
             pb = sbuf([P, W], F32, "pb%d" % t)
             nc.scalar.activation(pa[:], y[t][:].indirect(n1_t[:]), COPY)
             nc.scalar.activation(pb[:], y[t][:].indirect(n2_t[:]), COPY)
-            if t == 2:
-                d_plane = pick_dictionary()
-                ra.append(shared.tile([P, W], F32, name="ra2", offset=4 * G - 4 * W, align_bytes=64))
+            if t == 0:
+                ra.append(sbuf([P, W], F32, "ra0"))
             else:
-                ra.append(sbuf([P, W], F32, "ra%d" % t))
+                ra.append(shared.tile([P, W], F32, name="ra%d" % t, offset=2 * S * PACK + 4 * W * t, align_bytes=64))
             nc.vector.tensor_tensor(ra[t][:], pa[:], pb[:], MAX)
+            if t == 0:
+                d_plane = pick_dictionary()
 
         halves = [slice(0, S // 2), slice(S // 2, S)]
         z = [

@@ -98,17 +98,22 @@ def tile_picked_dhqfillsendtwo_none_p_kernel(
         gain = shared.tile([P, PACK], F32, name="gain", offset=4 * G, align_bytes=64)
         nc.sync.dma_start(gain[:], gs.rearrange("(p t) o -> p (t o)", t=PACK))
 
-        w_codes = [[sbuf([P, P], U32, "w_codes%d_%d" % (a, t)) for t in range(PACK)] for a in range(2)]
+        w_first = [sbuf([P, P], U32, "w_first%d" % a) for a in range(2)]
+        w_rest = [sbuf([P, PACK - 1, P], U32, "w_rest%d" % a) for a in range(2)]
+        w_codes = [[w_first[a][:]] + [w_rest[a][:, t, :] for t in range(PACK - 1)] for a in range(2)]
         y_bank = [psum.tile([P, S], F32, name="y_bank%d" % t, tag="y_bank%d" % t) for t in range(PACK)]
         y = [sbuf([P, S], F32, "y%d" % t) for t in range(PACK)]
-        for t in range(PACK):
-            for a in range(2):
-                nc.scalar.copy(w_codes[a][t][:], w_words[a][:, t:H:PACK])
+        for a in range(2):
+            nc.scalar.copy(w_first[a][:], w_words[a][:, 0:H:PACK])
+            nc.scalar.copy(
+                w_rest[a][:].rearrange("p t m -> p m t"),
+                w_words[a][:].rearrange("p (m t) -> p m t", t=PACK)[:, :, 1:],
+            )
         for t in range(PACK):
             for a in range(2):
                 nc.tensor.matmul_mx(
                     out=y_bank[t][:],
-                    lhsT=w_codes[a][t][:].bitcast(FP8X4),
+                    lhsT=w_codes[a][t].bitcast(FP8X4),
                     lhsT_scale=w_plane[t][:, a, :],
                     rhs=x_codes[:, a * S : (a + 1) * S].bitcast(FP8X4),
                     rhs_scale=x_plane[:, a * S : (a + 1) * S],
@@ -143,12 +148,12 @@ def tile_picked_dhqfillsendtwo_none_p_kernel(
             pb = sbuf([P, W], F32, "pb%d" % t)
             nc.scalar.activation(pa[:], y[t][:].indirect(n1_t[:]), COPY)
             nc.scalar.activation(pb[:], y[t][:].indirect(n2_t[:]), COPY)
-            if t == 0:
-                ra.append(sbuf([P, W], F32, "ra0"))
+            if t < 2:
+                ra.append(sbuf([P, W], F32, "ra%d" % t))
             else:
                 ra.append(shared.tile([P, W], F32, name="ra%d" % t, offset=2 * S * PACK + 4 * W * t, align_bytes=64))
             nc.vector.tensor_tensor(ra[t][:], pa[:], pb[:], MAX)
-            if t == 0:
+            if t == 1:
                 d_plane = pick_dictionary()
 
         halves = [slice(0, S // 2), slice(S // 2, S)]

from contextlib import ExitStack

import concourse.mybir as mybir

FLOPS = 402653184

F32 = mybir.dt.float32
BF16 = mybir.dt.bfloat16
I32 = mybir.dt.int32
U32 = mybir.dt.uint32
U16 = mybir.dt.uint16
U8 = mybir.dt.uint8
FP8X4 = mybir.dt.float8_e4m3fn_x4
COPY = mybir.ActivationFunctionType.Copy
MULT = mybir.AluOpType.mult
MAX = mybir.AluOpType.max

P = 128
PACK = 4
T, S, H, W, G = 1024, 256, 512, 128, 2048
TILES = H // P


def words_of(dram_words):
    return dram_words[0].rearrange("p n t -> p (n t)").bitcast(I32)


def tile_picked_dhqfillsendtwo_none_p_kernel(
    tc, x_words, x_scales, w1_words, w1_scales, w2_words, w2_scales, gs, d_words, d_scales,
    offs, hz, n1, n2, k1, n3, n4, out,
):
    nc = tc.nc
    with ExitStack() as ctx:
        lists = ctx.enter_context(tc.tile_pool(name="lists", bufs=1))
        keep = ctx.enter_context(tc.tile_pool(name="keep", bufs=1))
        shared = ctx.enter_context(tc.tile_pool(name="shared", bufs=1))
        psum = ctx.enter_context(tc.psum_pool(name="psum", bufs=1))

        def load_list(dram, name):
            tile = lists.tile(list(dram.shape), U16, name=name)
            nc.sync.dma_start(tile[:], dram)
            return tile

        def sbuf(shape, dtype, name, tag=None):
            return keep.tile(shape, dtype, name=name, tag=tag or name, align_bytes=64)

        x_word_table = sbuf([P, T], U32, "x_word_table")
        x_byte_table = sbuf([P, T], U8, "x_byte_table")
        w_bytes = sbuf([P, 2 * H], U8, "w_bytes", tag="w_then_d_bytes")
        w_words = [sbuf([P, H], U32, "w_words%d" % a) for a in range(2)]

        def load_scale_rows(rows, scales):
            words = scales[0].bitcast(I32)
            nc.sync.dma_start(rows.bitcast(I32), words.unsqueeze(1).to_broadcast([16, 8, words.shape[1]]))

        def place_scale_rows(plane):
            words = plane[:].bitcast(I32)
            for j in range(1, 4):
                nc.sync.dma_start(words[j:P:32, :], words[8 * j : P : 32, :])

        load_scale_rows(x_byte_table[:], x_scales)
        offs_t = load_list(offs, "offs")
        hz_t = load_list(hz, "hz")
        load_scale_rows(w_bytes[:, :H], w1_scales)
        load_scale_rows(w_bytes[:, H:], w2_scales)
        n1_t = load_list(n1, "n1")
        n2_t = load_list(n2, "n2")
        nc.sync.dma_start(x_word_table[:].bitcast(I32), words_of(x_words))
        k1_t = load_list(k1, "k1")
        n3_t = load_list(n3, "n3")
        n4_t = load_list(n4, "n4")
        place_scale_rows(w_bytes)
        nc.gpsimd.dma_start(w_words[0][:].bitcast(I32), words_of(w1_words))
        nc.gpsimd.dma_start(w_words[1][:].bitcast(I32), words_of(w2_words))

        def plane_of(picked, name, width):
            plane = sbuf([P, width], U8, name)
            nc.vector.tensor_copy(plane[:].bitcast(I32), picked.bitcast(I32))
            place_scale_rows(plane)
            return plane

        x_bytes_wide = shared.tile([P, G + 192], U8, name="x_bytes_picked", offset=4 * G - 64, align_bytes=64)
        x_bytes_picked = x_bytes_wide[:, : 2 * S]
        for a, lst in enumerate((offs_t, hz_t)):
            nc.vector.tensor_copy(x_bytes_picked[:, a * S : (a + 1) * S], x_byte_table[:].indirect(lst[:]))
        x_plane = plane_of(x_bytes_picked, "x_plane", 2 * S)
        x_codes = shared.tile([P, 2 * S], U32, name="x_codes", offset=5 * G + 64, align_bytes=64)
        for a, lst in enumerate((offs_t, hz_t)):
            nc.vector.tensor_copy(x_codes[:, a * S : (a + 1) * S], x_word_table[:].indirect(lst[:]))

        w_plane = [sbuf([P, 2, P], U8, "w_plane%d" % t) for t in range(PACK)]
        for t in range(PACK):
            nc.vector.tensor_copy(w_plane[t][:], w_bytes[:].rearrange("p (a m t) -> p t a m", a=2, t=PACK)[:, t])
        d_byte_table = shared.tile([P, G], U8, name="d_byte_table", offset=4 * G + 64, align_bytes=64)
        load_scale_rows(d_byte_table[:], d_scales)
        d_word_table = shared.tile([P, G], U32, name="d_word_table", offset=0, align_bytes=64)
        nc.sync.dma_start(d_word_table[:].bitcast(I32), words_of(d_words))
        gain = shared.tile([P, PACK], F32, name="gain", offset=4 * G, align_bytes=64)
        nc.sync.dma_start(gain[:], gs.rearrange("(p t) o -> p (t o)", t=PACK))

        w_first = [sbuf([P, P], U32, "w_first%d" % a) for a in range(2)]
        w_rest = [sbuf([P, PACK - 1, P], U32, "w_rest%d" % a) for a in range(2)]
        w_codes = [[w_first[a][:]] + [w_rest[a][:, t, :] for t in range(PACK - 1)] for a in range(2)]
        y_bank = [psum.tile([P, S], F32, name="y_bank%d" % t, tag="y_bank%d" % t) for t in range(PACK)]
        y = [sbuf([P, S], F32, "y%d" % t) for t in range(PACK)]
        for a in range(2):
            nc.scalar.copy(w_first[a][:], w_words[a][:, 0:H:PACK])
            nc.scalar.copy(
                w_rest[a][:].rearrange("p t m -> p m t"),
                w_words[a][:].rearrange("p (m t) -> p m t", t=PACK)[:, :, 1:],
            )
        for t in range(PACK):
            for a in range(2):
                nc.tensor.matmul_mx(
                    out=y_bank[t][:],
                    lhsT=w_codes[a][t].bitcast(FP8X4),
                    lhsT_scale=w_plane[t][:, a, :],
                    rhs=x_codes[:, a * S : (a + 1) * S].bitcast(FP8X4),
                    rhs_scale=x_plane[:, a * S : (a + 1) * S],
                    start=(a == 0),
                    stop=(a == 1),
                )
        nc.scalar.copy(y[0][:], y_bank[0][:])
        for t in range(1, PACK):
            nc.vector.tensor_copy(y[t][:], y_bank[t][:])

        d_bytes_picked = sbuf([P, H], U8, "d_bytes_picked", tag="w_then_d_bytes")
        d_codes = sbuf([P, H], U32, "d_codes")
        half = H // 2

        def pick_dictionary():
            for b in range(2):
                nc.vector.tensor_copy(
                    d_bytes_picked[:, b * half : (b + 1) * half],
                    d_byte_table[:].indirect(k1_t[:, b * half // 16 : (b + 1) * half // 16]),
                )
            plane = plane_of(d_bytes_picked[:], "d_plane", H)
            for b in range(2):
                nc.vector.tensor_copy(
                    d_codes[:, b * half : (b + 1) * half],
                    d_word_table[:].indirect(k1_t[:, b * half // 16 : (b + 1) * half // 16]),
                )
            return plane

        ra = []
        for t in range(PACK):
            pa = sbuf([P, W], F32, "pa%d" % t)
            pb = sbuf([P, W], F32, "pb%d" % t)
            nc.scalar.activation(pa[:], y[t][:].indirect(n1_t[:]), COPY)
            nc.scalar.activation(pb[:], y[t][:].indirect(n2_t[:]), COPY)
            if t < 2:
                ra.append(sbuf([P, W], F32, "ra%d" % t))
            else:
                ra.append(shared.tile([P, W], F32, name="ra%d" % t, offset=2 * S * PACK + 4 * W * t, align_bytes=64))
            nc.vector.tensor_tensor(ra[t][:], pa[:], pb[:], MAX)
            if t == 1:
                d_plane = pick_dictionary()

        halves = [slice(0, S // 2), slice(S // 2, S)]
        z = [
            shared.tile([P, S // 2, PACK], BF16, name="z%d" % b, offset=b * S * PACK, align_bytes=64) for b in range(2)
        ]
        for t in range(PACK):
            nc.scalar.activation(y[t][:].indirect(n1_t[:]), ra[t][:], COPY)
            for b in range(2):
                nc.vector.tensor_scalar(z[b][:, :, t], y[t][:, halves[b]], gain[:, t : t + 1], None, MULT)
        z_codes = sbuf([P, S], U32, "z_codes")
        z_plane = sbuf([P, S], U8, "z_plane")
        for b in range(2):
            nc.vector.quantize_mx(
                out=z_codes[:, halves[b]].bitcast(FP8X4),
                scales=z_plane[:, halves[b]],
                in_=z[b][:].rearrange("p s t -> p (s t)"),
            )

        def coded_product(u, bank, places):
            cols = slice(u * P, (u + 1) * P)
            nc.tensor.matmul_mx(
                out=bank,
                lhsT=d_codes[:, cols].bitcast(FP8X4),
                lhsT_scale=d_plane[:, cols],
                rhs=z_codes[:, places].bitcast(FP8X4),
                rhs_scale=z_plane[:, places],
                start=True,
                stop=True,
            )

        for u in range(TILES):
            h = sbuf([P, S], F32, "h%d" % u)
            sent3 = sbuf([P, 2 * S], F32, "sent3_%d" % u)
            sent4 = sbuf([P, 2 * S], F32, "sent4_%d" % u)
            if u == 0:
                for b in range(2):
                    bank = psum.tile([P, S], F32, name="h_first%d" % b, tag="y_bank%d" % b)
                    coded_product(u, bank[:, : S // 2], halves[b])
                    if b == 0:
                        nc.scalar.activation(h[:, halves[b]], bank[:, : S // 2], COPY, scale=0.0625)
                    else:
                        nc.vector.tensor_scalar(h[:, halves[b]], bank[:, : S // 2], 0.0625, None, MULT)
                    nc.scalar.activation(sent3[:].indirect(n3_t[:, b * 8 : (b + 1) * 8]), h[:, halves[b]], COPY)
            else:
                bank = psum.tile([P, S], F32, name="h_bank%d" % u)
                coded_product(u, bank[:], slice(0, S))
                nc.vector.tensor_scalar(h[:], bank[:], 0.0625, None, MULT)
                nc.scalar.activation(sent3[:].indirect(n3_t[:]), h[:], COPY)
            nc.scalar.activation(sent4[:].indirect(n4_t[:]), h[:], COPY)
            larger = sbuf([P, S], F32, "larger%d" % u)
            rows = out[u * P : (u + 1) * P, :]
            if u < TILES - 1:
                nc.vector.tensor_tensor(larger[:], sent3[:, :S], sent4[:, :S], MAX)
                nc.sync.dma_start(rows, larger[:])
            else:
                for b, queue in enumerate((nc.sync, nc.scalar)):
                    nc.vector.tensor_tensor(larger[:, halves[b]], sent3[:, halves[b]], sent4[:, halves[b]], MAX)
                    queue.dma_start(rows[:, halves[b]], larger[:, halves[b]])
